import numpy as np
import ml_dtypes


def mxq(x, axis, fmt="e4m3"):
    dtype, down = {"e4m3": (ml_dtypes.float8_e4m3fn, 7), "e5m2": (ml_dtypes.float8_e5m2, 14)}[fmt]
    v = np.moveaxis(np.asarray(x, np.float32).astype(ml_dtypes.bfloat16).astype(np.float64), axis, -1)
    blocks = v.reshape(v.shape[:-1] + (-1, 32))
    amax = np.abs(blocks).max(-1, keepdims=True)
    byte = np.maximum(np.where(amax > 0, np.frexp(amax)[1] - 1 + 127, 0) - down, 1)
    scale = np.exp2(byte - 127.0)
    codes = (blocks / scale).astype(np.float32).astype(dtype).astype(np.float64)
    return np.moveaxis((codes * scale).reshape(v.shape), -1, axis)


WIDE = False


def mx_kscale(k):
    if not WIDE:
        return np.ones(k)
    levels = np.array([10, -10, 5, -5, 0])
    if k % 512:
        return np.exp2(np.random.permutation(np.resize(levels, k // 32))).repeat(32)
    a = np.empty((k // 512, 16))
    for p in range(k // 512):
        a[p, :8] = np.random.permutation(np.resize(levels, 8))
        for g in range(8):
            far = levels[np.abs(levels - a[p, g]) >= 10]
            a[p, g + 8] = far[np.random.randint(len(far))]
    return np.exp2(a.ravel()).repeat(32)


def f64(x):
    return np.asarray(x).astype(np.float64)


def striped(idx):
    return np.tile(idx.reshape(-1, 16).T, (8, 1)).astype(np.uint16)


def unstriped(offs):
    return offs[:16].T.reshape(-1).astype(np.int64)


def pack_weight(w):
    k, n = w.shape
    w = f64(np.asarray(w, np.float32).astype(ml_dtypes.bfloat16)).reshape(k // 32, 32, n)
    amax = np.abs(w).max(1)
    byte = np.clip(np.where(amax > 0, np.frexp(amax)[1] - 1 + 127 - 7, 1), 1, 254)
    scaled = (w * np.exp2(127.0 - byte)[:, None, :]).reshape(k, n).astype(np.float32)
    words = np.ascontiguousarray(scaled.reshape(k // 512, 128, 4, n).transpose(0, 1, 3, 2)).astype(ml_dtypes.float8_e4m3fn).view(np.uint8)
    return words, np.ascontiguousarray(byte.astype(np.uint8).reshape(k // 512, 16, n))


def unpack_weight(words, scales):
    g, p, n, _ = words.shape
    vals = np.ascontiguousarray(words).view(ml_dtypes.float8_e4m3fn).astype(np.float64) * np.repeat(np.exp2(scales.astype(np.float64) - 127.0), 8, axis=1)[..., None]
    return vals.transpose(0, 1, 3, 2).reshape(g * 512, n)


K, T, S, D, N, H, V, U = 512, 4096, 1024, 4, 128, 512, 256, 512


def setup_inputs():
    n = np.random.standard_normal
    s = mx_kscale(K)[:, None]
    u = mx_kscale(H)
    packed_xT = pack_weight(n((K, T)) * s)
    return {
        "x_words": packed_xT[0],
        "x_scales": packed_xT[1],
        "w1": (n((K, H)) / np.sqrt(K) / s).astype(np.float32),
        "st": (np.random.uniform(0.6, 1.4, (H, S))).astype(np.float32),
        "unit": (np.random.uniform(0.6, 1.4, (H, 1)) * u[:, None]).astype(np.float32),
        "w2": (n((H, N)) / np.sqrt(H) / u[:, None]).astype(np.float32),
        "offs": striped(np.random.permutation(T)[:S]),
        "mv": striped(np.random.permutation(S)),
        "out_t": striped(np.random.permutation(np.concatenate([np.arange(V), np.random.randint(0, V, U - V)]))),
    }


def reference(x_words, x_scales, w1, st, unit, w2, offs, mv, out_t):
    xq = unpack_weight(x_words, x_scales)[:, unstriped(offs)]
    y = mxq(f64(w1), 0, "e4m3").T @ xq
    ym = y[:, unstriped(mv)]
    flat = ym * f64(st)
    stack = flat.reshape(len(flat), -1, D).sum(axis=2)
    t2 = (flat) ** 2
    energ = t2.reshape(len(t2), -1, D).sum(axis=2)
    semb = ((stack) ** 2) / (4.0 * energ + 0.5)
    sbu = semb[:, unstriped(out_t)]
    wst = stack[:, unstriped(out_t)] * sbu
    hid = f64(unit) * wst
    return mxq(f64(w2), 0, "e4m3").T @ mxq(hid, 0, "e4m3")

@@ -1,0 +1,190 @@
+from contextlib import ExitStack
+
+import concourse.mybir as mybir
+from concourse.masks import make_identity
+
+K, T, S, D, N, H, V, U = 512, 4096, 1024, 4, 128, 512, 256, 512
+FLOPS = 2 * K * H * S + 2 * H * N * U
+
+F32 = mybir.dt.float32
+BF16 = mybir.dt.bfloat16
+I32 = mybir.dt.int32
+U32 = mybir.dt.uint32
+U16 = mybir.dt.uint16
+U8 = mybir.dt.uint8
+FP8X4 = mybir.dt.float8_e4m3fn_x4
+ALU = mybir.AluOpType
+ACT = mybir.ActivationFunctionType
+AXIS = mybir.AxisListType
+
+P = 128
+PACK = 4
+HALF = S // 2
+VB = HALF // D
+RH = U // 2
+
+
+def tile_picked_ysembl_wst_p_kernel(
+    tc, x_words, x_scales, w1, st, unit, w2, offs, mv, out_t, out
+):
+    nc = tc.nc
+    with ExitStack() as ctx:
+        keep = ctx.enter_context(tc.tile_pool(name="keep", bufs=1))
+        ring = ctx.enter_context(tc.tile_pool(name="ring", bufs=4))
+        psum_y = ctx.enter_context(tc.psum_pool(name="psum_y", bufs=4))
+        psum_e = ctx.enter_context(tc.psum_pool(name="psum_e", bufs=2))
+
+        offs_sb = keep.tile([P, S // 16], U16, name="offs_sb")
+        mv_sb = keep.tile([P, S // 16], U16, name="mv_sb")
+        out_t_sb = keep.tile([P, U // 16], U16, name="out_t_sb")
+        words = keep.tile([P, T], I32, name="words", align_bytes=64)
+        scales = keep.tile([P, T], U8, name="scales", align_bytes=64)
+        w1_raw = [keep.tile([P, PACK, H // 2], F32, name=f"w1_raw{c}") for c in range(2)]
+        w2_raw = keep.tile([P, PACK, N], F32, name="w2_raw")
+        unit_sb = keep.tile([P, PACK], F32, name="unit_sb")
+        st_sb = [keep.tile([P, S], F32, name=f"st{t}") for t in range(PACK)]
+        ident = keep.tile([P, P], F32, name="ident")
+
+        nc.vector.memset(scales[:].bitcast(I32), 0)
+        nc.sync.dma_start(offs_sb[:], offs)
+        nc.sync.dma_start(words[:], x_words[0].rearrange("p n t -> p (n t)").bitcast(I32))
+        for q in range(4):
+            nc.scalar.dma_start(
+                scales[32 * q : 32 * q + 4, :].bitcast(I32), x_scales[0][4 * q : 4 * q + 4, :].bitcast(I32)
+            )
+        w1_rows = w1.rearrange("(p j) c -> p j c", j=PACK)
+        for c in range(2):
+            nc.sync.dma_start(w1_raw[c][:], w1_rows[:, :, c * (H // 2) : (c + 1) * (H // 2)])
+        st_rows = st.rearrange("(p t) j -> p t j", t=PACK)
+        nc.sync.dma_start(mv_sb[:], mv)
+        nc.sync.dma_start(st_sb[0][:], st_rows[:, 0, :])
+        nc.sync.dma_start(st_sb[1][:], st_rows[:, 1, :])
+        nc.sync.dma_start(unit_sb[:], unit.rearrange("(p t) o -> p (t o)", t=PACK))
+        nc.sync.dma_start(out_t_sb[:], out_t)
+        nc.sync.dma_start(w2_raw[:], w2.rearrange("(p j) m -> p j m", j=PACK))
+        nc.sync.dma_start(st_sb[2][:], st_rows[:, 2, :])
+        nc.sync.dma_start(st_sb[3][:], st_rows[:, 3, :])
+        make_identity(nc, ident[:])
+
+        x_bytes = keep.tile([P, S], U8, name="x_bytes", align_bytes=64)
+        nc.vector.tensor_copy(x_bytes[:], scales[:].indirect(offs_sb[:]))
+        x_codes = [keep.tile([P, HALF], U32, name=f"x_codes{h}", align_bytes=64) for h in range(2)]
+        for h in range(2):
+            nc.vector.tensor_copy(
+                x_codes[h][:], words[:].bitcast(U32).indirect(offs_sb[:, h * (HALF // 16) : (h + 1) * (HALF // 16)])
+            )
+
+        w1_bf = keep.tile([P, PACK, P, PACK], BF16, name="w1_bf", align_bytes=64)
+        for c in range(2):
+            dst = w1_bf[:, :, c * (P // 2) : (c + 1) * (P // 2), :].rearrange("p t m j -> p m t j")
+            src = w1_raw[c][:].rearrange("p j (m t) -> p m t j", t=PACK)
+            if c == 0:
+                nc.scalar.copy(dst, src)
+            else:
+                nc.vector.tensor_copy(dst, src)
+        w1_codes = keep.tile([P, H], U32, name="w1_codes", align_bytes=64)
+        w1_scales = keep.tile([P, H], U8, name="w1_scales", align_bytes=64)
+        w1_flat = w1_bf[:].rearrange("p t m j -> p (t m j)")
+        for a, b in ((0, P), (P, H)):
+            nc.vector.quantize_mx(
+                out=w1_codes[:, a:b].bitcast(FP8X4), scales=w1_scales[:, a:b], in_=w1_flat[:, PACK * a : PACK * b]
+            )
+
+        y_sb = [keep.tile([P, S], F32, name=f"y{t}") for t in range(PACK)]
+        for t in range(PACK):
+            for h in range(2):
+                acc = psum_y.tile([P, HALF], F32, name="acc")
+                nc.tensor.matmul_mx(
+                    out=acc[:],
+                    lhsT=w1_codes[:, t * P : (t + 1) * P].bitcast(FP8X4),
+                    lhsT_scale=w1_scales[:, t * P : (t + 1) * P],
+                    rhs=x_codes[h][:].bitcast(FP8X4),
+                    rhs_scale=x_bytes[:, h * HALF : (h + 1) * HALF],
+                    start=True,
+                    stop=True,
+                )
+                if (t, h) == (0, 1):
+                    nc.vector.tensor_copy(y_sb[t][:, h * HALF : (h + 1) * HALF], acc[:])
+                else:
+                    nc.scalar.copy(y_sb[t][:, h * HALF : (h + 1) * HALF], acc[:])
+
+        w2_bf = keep.tile([P, N, PACK], BF16, name="w2_bf", align_bytes=64)
+        nc.scalar.copy(
+            w2_bf[:].rearrange("p (c i) j -> p c j i", i=4), w2_raw[:].rearrange("p j (c i) -> p c j i", i=4)
+        )
+        w2_codes = keep.tile([P, N], U32, name="w2_codes", align_bytes=64)
+        w2_scales = keep.tile([P, N], U8, name="w2_scales", align_bytes=64)
+        nc.vector.quantize_mx(
+            out=w2_codes[:].bitcast(FP8X4), scales=w2_scales[:], in_=w2_bf[:].rearrange("p m j -> p (m j)")
+        )
+
+        hid_rows = [keep.tile([P, PACK, RH], BF16, name=f"hid_rows{r}") for r in range(2)]
+        for t in range(PACK):
+            table = keep.tile([P, 4 * V], F32, name=f"table{t}")
+            weighted, stack, ratio, semb = (table[:, n * V : (n + 1) * V] for n in range(4))
+            energ_t = psum_e.tile([P, 2, P], F32, name="energ_t")
+            for h in range(2):
+                flat = ring.tile([P, HALF], F32, name="flat")
+                nc.vector.tensor_tensor(
+                    flat[:],
+                    y_sb[t][:].indirect(mv_sb[:, h * (HALF // 16) : (h + 1) * (HALF // 16)]),
+                    st_sb[t][:, h * HALF : (h + 1) * HALF],
+                    ALU.mult,
+                )
+                squares = ring.tile([P, D, VB], F32, name="squares")
+                nc.scalar.activation(
+                    squares[:].rearrange("p d (b q) -> p b d q", q=4),
+                    flat[:].rearrange("p (b q d) -> p b d q", q=4, d=D),
+                    ACT.Square,
+                )
+                nc.vector.tensor_reduce(
+                    stack[:, h * VB : (h + 1) * VB], flat[:].rearrange("p (v d) -> p v d", d=D), AXIS.X, ALU.add
+                )
+                for d in range(D):
+                    nc.tensor.matmul(
+                        energ_t[:, h, :],
+                        lhsT=squares[:, d, :],
+                        rhs=ident[:],
+                        start=(d == 0),
+                        stop=(d == D - 1),
+                        is_transpose=True,
+                    )
+            root_t = ring.tile([P, 2, P], F32, name="root_t")
+            nc.scalar.activation(root_t[:], energ_t[:], ACT.Abs_reciprocal_sqrt, bias=0.5, scale=4.0)
+            root = psum_e.tile([P, V], F32, name="root")
+            for h in range(2):
+                nc.tensor.transpose(root[:, h * VB : (h + 1) * VB], root_t[:, h, :], ident[:])
+            nc.vector.tensor_tensor(ratio, stack, root[:], ALU.mult)
+            nc.scalar.activation(semb, ratio, ACT.Square)
+            nc.vector.scalar_tensor_tensor(weighted, semb, unit_sb[:, t : t + 1], stack, ALU.mult, ALU.mult)
+            for r in range(2):
+                picked = table[:].indirect(out_t_sb[:, r * (RH // 16) : (r + 1) * (RH // 16)])
+                if t == PACK - 1 and r == 0:
+                    nc.vector.tensor_copy(hid_rows[r][:, t, :], picked)
+                else:
+                    nc.scalar.activation(hid_rows[r][:, t, :], picked, ACT.Copy)
+
+        for r in range(2):
+            hid_bf = keep.tile([P, RH, PACK], BF16, name=f"hid_bf{r}", align_bytes=64)
+            nc.vector.tensor_copy(
+                hid_bf[:].rearrange("p (c i) t -> p c t i", i=4),
+                hid_rows[r][:].rearrange("p t (c i) -> p c t i", i=4),
+            )
+            hid_codes = keep.tile([P, RH], U32, name=f"hid_codes{r}", align_bytes=64)
+            hid_scales = keep.tile([P, RH], U8, name=f"hid_scales{r}", align_bytes=64)
+            nc.vector.quantize_mx(
+                out=hid_codes[:].bitcast(FP8X4), scales=hid_scales[:], in_=hid_bf[:].rearrange("p r t -> p (r t)")
+            )
+            acc = psum_y.tile([P, RH], F32, name="acc")
+            nc.tensor.matmul_mx(
+                out=acc[:],
+                lhsT=w2_codes[:].bitcast(FP8X4),
+                lhsT_scale=w2_scales[:],
+                rhs=hid_codes[:].bitcast(FP8X4),
+                rhs_scale=hid_scales[:],
+                start=True,
+                stop=True,
+            )
+            result = keep.tile([P, RH], F32, name=f"result{r}")
+            nc.scalar.copy(result[:], acc[:])
+            nc.sync.dma_start(out[:, r * RH : (r + 1) * RH], result[:])

@@ -24,14 +24,18 @@ VB = HALF // D
 RH = U // 2
 
 
+def entries(lst, a, b):
+    return lst[:, a // 16 : b // 16]
+
+
 def tile_picked_ysembl_wst_p_kernel(
     tc, x_words, x_scales, w1, st, unit, w2, offs, mv, out_t, out
 ):
     nc = tc.nc
     with ExitStack() as ctx:
         keep = ctx.enter_context(tc.tile_pool(name="keep", bufs=1))
-        ring = ctx.enter_context(tc.tile_pool(name="ring", bufs=4))
-        psum_y = ctx.enter_context(tc.psum_pool(name="psum_y", bufs=4))
+        ring = ctx.enter_context(tc.tile_pool(name="ring", bufs=2))
+        psum_y = ctx.enter_context(tc.psum_pool(name="psum_y", bufs=3))
         psum_e = ctx.enter_context(tc.psum_pool(name="psum_e", bufs=2))
 
         offs_sb = keep.tile([P, S // 16], U16, name="offs_sb")
@@ -41,132 +45,194 @@ def tile_picked_ysembl_wst_p_kernel(
         scales = keep.tile([P, T], U8, name="scales", align_bytes=64)
         w1_raw = [keep.tile([P, PACK, H // 2], F32, name=f"w1_raw{c}") for c in range(2)]
         w2_raw = keep.tile([P, PACK, N], F32, name="w2_raw")
+        gains = [keep.tile([P, S], F32, name=f"gains{t}") for t in range(PACK)]
         unit_sb = keep.tile([P, PACK], F32, name="unit_sb")
-        st_sb = [keep.tile([P, S], F32, name=f"st{t}") for t in range(PACK)]
         ident = keep.tile([P, P], F32, name="ident")
 
         nc.vector.memset(scales[:].bitcast(I32), 0)
         nc.sync.dma_start(offs_sb[:], offs)
-        nc.sync.dma_start(words[:], x_words[0].rearrange("p n t -> p (n t)").bitcast(I32))
-        for q in range(4):
-            nc.scalar.dma_start(
-                scales[32 * q : 32 * q + 4, :].bitcast(I32), x_scales[0][4 * q : 4 * q + 4, :].bitcast(I32)
-            )
         w1_rows = w1.rearrange("(p j) c -> p j c", j=PACK)
         for c in range(2):
             nc.sync.dma_start(w1_raw[c][:], w1_rows[:, :, c * (H // 2) : (c + 1) * (H // 2)])
-        st_rows = st.rearrange("(p t) j -> p t j", t=PACK)
+        for q in range(4):
+            nc.sync.dma_start(
+                scales[32 * q : 32 * q + 4, :].bitcast(I32), x_scales[0][4 * q : 4 * q + 4, :].bitcast(I32)
+            )
+        nc.sync.dma_start(words[:], x_words[0].rearrange("p n t -> p (n t)").bitcast(I32))
         nc.sync.dma_start(mv_sb[:], mv)
-        nc.sync.dma_start(st_sb[0][:], st_rows[:, 0, :])
-        nc.sync.dma_start(st_sb[1][:], st_rows[:, 1, :])
-        nc.sync.dma_start(unit_sb[:], unit.rearrange("(p t) o -> p (t o)", t=PACK))
-        nc.sync.dma_start(out_t_sb[:], out_t)
         nc.sync.dma_start(w2_raw[:], w2.rearrange("(p j) m -> p j m", j=PACK))
-        nc.sync.dma_start(st_sb[2][:], st_rows[:, 2, :])
-        nc.sync.dma_start(st_sb[3][:], st_rows[:, 3, :])
+        st_rows = st.rearrange("(p t) j -> p t j", t=PACK)
+        for t in (0, 1):
+            nc.sync.dma_start(gains[t][:], st_rows[:, t, :])
+        nc.sync.dma_start(out_t_sb[:], out_t)
+        nc.sync.dma_start(unit_sb[:], unit.rearrange("(p t) o -> p (t o)", t=PACK))
+        for t in (2, 3):
+            nc.sync.dma_start(gains[t][:], st_rows[:, t, :])
         make_identity(nc, ident[:])
 
-        x_bytes = keep.tile([P, S], U8, name="x_bytes", align_bytes=64)
-        nc.vector.tensor_copy(x_bytes[:], scales[:].indirect(offs_sb[:]))
-        x_codes = [keep.tile([P, HALF], U32, name=f"x_codes{h}", align_bytes=64) for h in range(2)]
-        for h in range(2):
-            nc.vector.tensor_copy(
-                x_codes[h][:], words[:].bitcast(U32).indirect(offs_sb[:, h * (HALF // 16) : (h + 1) * (HALF // 16)])
-            )
+        warm = keep.tile([P, 1], F32, name="warm")
+        nc.scalar.activation(warm[:], ident[:, 0:1], ACT.Abs_reciprocal_sqrt, bias=0.5, scale=4.0)
 
         w1_bf = keep.tile([P, PACK, P, PACK], BF16, name="w1_bf", align_bytes=64)
-        for c in range(2):
-            dst = w1_bf[:, :, c * (P // 2) : (c + 1) * (P // 2), :].rearrange("p t m j -> p m t j")
-            src = w1_raw[c][:].rearrange("p j (m t) -> p m t j", t=PACK)
-            if c == 0:
-                nc.scalar.copy(dst, src)
-            else:
-                nc.vector.tensor_copy(dst, src)
+        for c, move in enumerate((nc.scalar.copy, nc.vector.tensor_copy)):
+            move(
+                w1_bf[:, :, c * (P // 2) : (c + 1) * (P // 2), :].rearrange("p t m j -> p m t j"),
+                w1_raw[c][:].rearrange("p j (m t) -> p m t j", t=PACK),
+            )
         w1_codes = keep.tile([P, H], U32, name="w1_codes", align_bytes=64)
         w1_scales = keep.tile([P, H], U8, name="w1_scales", align_bytes=64)
-        w1_flat = w1_bf[:].rearrange("p t m j -> p (t m j)")
-        for a, b in ((0, P), (P, H)):
-            nc.vector.quantize_mx(
-                out=w1_codes[:, a:b].bitcast(FP8X4), scales=w1_scales[:, a:b], in_=w1_flat[:, PACK * a : PACK * b]
-            )
+        nc.vector.quantize_mx(
+            out=w1_codes[:].bitcast(FP8X4), scales=w1_scales[:], in_=w1_bf[:].rearrange("p t m j -> p (t m j)")
+        )
+
+        pieces = ((0, HALF), (HALF, 3 * S // 4), (3 * S // 4, S))
+        x_bytes = keep.tile([P, S], U8, name="x_bytes", align_bytes=64)
+        nc.vector.tensor_copy(x_bytes[:], scales[:].indirect(offs_sb[:]))
+        x_codes = keep.tile([P, S], U32, name="x_codes", align_bytes=64)
+        for a, b in pieces:
+            nc.vector.tensor_copy(x_codes[:, a:b], words[:].bitcast(U32).indirect(entries(offs_sb, a, b)))
 
         y_sb = [keep.tile([P, S], F32, name=f"y{t}") for t in range(PACK)]
-        for t in range(PACK):
-            for h in range(2):
-                acc = psum_y.tile([P, HALF], F32, name="acc")
+        flats = [keep.tile([P, S], F32, name=f"flat{t}") for t in range(PACK)]
+        tables = [keep.tile([P, 4 * V], F32, name=f"table{t}") for t in range(PACK)]
+        hid_rows = [keep.tile([P, PACK, RH], BF16, name=f"hid_rows{r}") for r in range(2)]
+        ON_PE = (0, 1)
+        sums_t = {}
+
+        def project(t):
+            for a, b in pieces if t == 0 else ((0, HALF), (HALF, S)):
+                acc = psum_y.tile([P, b - a], F32, name="acc")
                 nc.tensor.matmul_mx(
                     out=acc[:],
                     lhsT=w1_codes[:, t * P : (t + 1) * P].bitcast(FP8X4),
                     lhsT_scale=w1_scales[:, t * P : (t + 1) * P],
-                    rhs=x_codes[h][:].bitcast(FP8X4),
-                    rhs_scale=x_bytes[:, h * HALF : (h + 1) * HALF],
+                    rhs=x_codes[:, a:b].bitcast(FP8X4),
+                    rhs_scale=x_bytes[:, a:b],
                     start=True,
                     stop=True,
                 )
-                if (t, h) == (0, 1):
-                    nc.vector.tensor_copy(y_sb[t][:, h * HALF : (h + 1) * HALF], acc[:])
+                if t == 0 and b == S:
+                    nc.vector.tensor_copy(y_sb[t][:, a:b], acc[:])
                 else:
-                    nc.scalar.copy(y_sb[t][:, h * HALF : (h + 1) * HALF], acc[:])
+                    nc.scalar.copy(y_sb[t][:, a:b], acc[:])
 
-        w2_bf = keep.tile([P, N, PACK], BF16, name="w2_bf", align_bytes=64)
-        nc.scalar.copy(
-            w2_bf[:].rearrange("p (c i) j -> p c j i", i=4), w2_raw[:].rearrange("p j (c i) -> p c j i", i=4)
-        )
-        w2_codes = keep.tile([P, N], U32, name="w2_codes", align_bytes=64)
-        w2_scales = keep.tile([P, N], U8, name="w2_scales", align_bytes=64)
-        nc.vector.quantize_mx(
-            out=w2_codes[:].bitcast(FP8X4), scales=w2_scales[:], in_=w2_bf[:].rearrange("p m j -> p (m j)")
-        )
+        def part(t, n):
+            return tables[t][:, n * V : (n + 1) * V]
 
-        hid_rows = [keep.tile([P, PACK, RH], BF16, name=f"hid_rows{r}") for r in range(2)]
-        for t in range(PACK):
-            table = keep.tile([P, 4 * V], F32, name=f"table{t}")
-            weighted, stack, ratio, semb = (table[:, n * V : (n + 1) * V] for n in range(4))
-            energ_t = psum_e.tile([P, 2, P], F32, name="energ_t")
-            for h in range(2):
-                flat = ring.tile([P, HALF], F32, name="flat")
-                nc.vector.tensor_tensor(
-                    flat[:],
-                    y_sb[t][:].indirect(mv_sb[:, h * (HALF // 16) : (h + 1) * (HALF // 16)]),
-                    st_sb[t][:, h * HALF : (h + 1) * HALF],
-                    ALU.mult,
+        def add_groups(dst, columns):
+            for d in range(D):
+                nc.tensor.matmul(
+                    dst, lhsT=columns(d), rhs=ident[:], start=(d == 0), stop=(d == D - 1), is_transpose=True
                 )
-                squares = ring.tile([P, D, VB], F32, name="squares")
-                nc.scalar.activation(
-                    squares[:].rearrange("p d (b q) -> p b d q", q=4),
-                    flat[:].rearrange("p (b q d) -> p b d q", q=4, d=D),
-                    ACT.Square,
-                )
-                nc.vector.tensor_reduce(
-                    stack[:, h * VB : (h + 1) * VB], flat[:].rearrange("p (v d) -> p v d", d=D), AXIS.X, ALU.add
-                )
-                for d in range(D):
-                    nc.tensor.matmul(
-                        energ_t[:, h, :],
-                        lhsT=squares[:, d, :],
-                        rhs=ident[:],
-                        start=(d == 0),
-                        stop=(d == D - 1),
-                        is_transpose=True,
-                    )
+
+        def moveout(t, h):
+            if h == 0:
+                sums_t[t] = psum_e.tile([P, 4, P], F32, name="sums_t", bufs=3)
+            a, b = h * HALF, (h + 1) * HALF
+            flat = flats[t][:, a:b]
+            nc.vector.tensor_tensor(flat, y_sb[t][:].indirect(entries(mv_sb, a, b)), gains[t][:, a:b], ALU.mult)
+            squares = ring.tile([P, HALF], F32, name="squares", bufs=4)
+            nc.scalar.activation(
+                squares[:].rearrange("p (e v f) -> p v e f", e=2, f=2),
+                flat.rearrange("p (v e f) -> p v e f", e=2, f=2),
+                ACT.Square,
+            )
+            column = lambda d: squares[:, (d // 2) * 2 * VB + d % 2 : (d // 2 + 1) * 2 * VB : 2]
+            if t in ON_PE:
+                add_groups(sums_t[t][:, 2 + h, :], lambda d: flat[:, d::D])
+            add_groups(sums_t[t][:, h, :], column)
+
+        def stack_up(t):
+            if t in ON_PE:
+                return
+            groups = flats[t][:].rearrange("p (v d) -> p v d", d=D)
+            pairs = ring.tile([P, V, 2], F32, name="pairs")
+            nc.vector.tensor_tensor(pairs[:], groups[:, :, 0:2], groups[:, :, 2:4], ALU.add)
+            nc.vector.tensor_tensor(part(t, 1), pairs[:, :, 0], pairs[:, :, 1], ALU.add)
+
+        def normalise(t):
             root_t = ring.tile([P, 2, P], F32, name="root_t")
-            nc.scalar.activation(root_t[:], energ_t[:], ACT.Abs_reciprocal_sqrt, bias=0.5, scale=4.0)
+            nc.scalar.activation(root_t[:], sums_t[t][:, 0:2, :], ACT.Abs_reciprocal_sqrt, bias=0.5, scale=4.0)
+            if t in ON_PE:
+                stack_t = sums_t[t][:, 2:4, :].rearrange("p a b -> p (a b)")
+                nc.vector.tensor_tensor(part(t, 2), root_t[:].rearrange("p a b -> p (a b)"), stack_t, ALU.mult)
+                return
             root = psum_e.tile([P, V], F32, name="root")
             for h in range(2):
                 nc.tensor.transpose(root[:, h * VB : (h + 1) * VB], root_t[:, h, :], ident[:])
-            nc.vector.tensor_tensor(ratio, stack, root[:], ALU.mult)
-            nc.scalar.activation(semb, ratio, ACT.Square)
-            nc.vector.scalar_tensor_tensor(weighted, semb, unit_sb[:, t : t + 1], stack, ALU.mult, ALU.mult)
-            for r in range(2):
-                picked = table[:].indirect(out_t_sb[:, r * (RH // 16) : (r + 1) * (RH // 16)])
-                if t == PACK - 1 and r == 0:
-                    nc.vector.tensor_copy(hid_rows[r][:, t, :], picked)
-                else:
-                    nc.scalar.activation(hid_rows[r][:, t, :], picked, ACT.Copy)
+            nc.vector.tensor_tensor(part(t, 2), part(t, 1), root[:], ALU.mult)
+
+        def weigh(t):
+            if t in (3,):
+                nc.vector.tensor_tensor(part(t, 3), part(t, 2), part(t, 2), ALU.mult)
+            else:
+                nc.scalar.activation(part(t, 3), part(t, 2), ACT.Square)
+            if t in ON_PE:
+                stack_t = sums_t[t][:, 2:4, :].rearrange("p a b -> p (a b)")
+                nc.vector.tensor_tensor(part(t, 1), part(t, 3), stack_t, ALU.mult)
+                back = psum_e.tile([P, V], F32, name="root")
+                for h in range(2):
+                    nc.tensor.transpose(back[:, h * VB : (h + 1) * VB], part(t, 1)[:, h * VB : (h + 1) * VB], ident[:])
+                nc.scalar.activation(part(t, 0), back[:], ACT.Copy, scale=unit_sb[:, t : t + 1])
+                return
+            nc.vector.scalar_tensor_tensor(part(t, 0), part(t, 3), unit_sb[:, t : t + 1], part(t, 1), ALU.mult, ALU.mult)
+
+        def look_up(t, r):
+            picked = tables[t][:].indirect(entries(out_t_sb, r * RH, (r + 1) * RH))
+            if (t, r) in ((3, 0),):
+                nc.vector.tensor_copy(hid_rows[r][:, t, :], picked)
+            else:
+                nc.scalar.activation(hid_rows[r][:, t, :], picked, ACT.Copy)
+
+        w2_bf = keep.tile([P, N, PACK], BF16, name="w2_bf", align_bytes=64)
+        w2_codes = keep.tile([P, N], U32, name="w2_codes", align_bytes=64)
+        w2_scales = keep.tile([P, N], U8, name="w2_scales", align_bytes=64)
+
+        def second_weights():
+            nc.scalar.copy(
+                w2_bf[:].rearrange("p (c i) j -> p c j i", i=4), w2_raw[:].rearrange("p j (c i) -> p c j i", i=4)
+            )
+            nc.vector.quantize_mx(
+                out=w2_codes[:].bitcast(FP8X4), scales=w2_scales[:], in_=w2_bf[:].rearrange("p m j -> p (m j)")
+            )
+
+        project(0)
+        project(1)
+        second_weights()
+        moveout(0, 0)
+        moveout(0, 1)
+        project(2)
+        moveout(1, 0)
+        moveout(1, 1)
+        project(3)
+        stack_up(0)
+        normalise(0)
+        weigh(0)
+        look_up(0, 0)
+        look_up(0, 1)
+        moveout(2, 0)
+        moveout(2, 1)
+        stack_up(1)
+        normalise(1)
+        weigh(1)
+        look_up(1, 0)
+        look_up(1, 1)
+        moveout(3, 0)
+        moveout(3, 1)
+        stack_up(2)
+        normalise(2)
+        weigh(2)
+        look_up(2, 0)
+        look_up(2, 1)
+        stack_up(3)
+        normalise(3)
+        weigh(3)
+        look_up(3, 0)
+        look_up(3, 1)
 
         for r in range(2):
             hid_bf = keep.tile([P, RH, PACK], BF16, name=f"hid_bf{r}", align_bytes=64)
-            nc.vector.tensor_copy(
+            (nc.scalar.copy if r in () else nc.vector.tensor_copy)(
                 hid_bf[:].rearrange("p (c i) t -> p c t i", i=4),
                 hid_rows[r][:].rearrange("p t (c i) -> p c t i", i=4),
             )
@@ -186,5 +252,5 @@ def tile_picked_ysembl_wst_p_kernel(
                 stop=True,
             )
             result = keep.tile([P, RH], F32, name=f"result{r}")
-            nc.scalar.copy(result[:], acc[:])
+            (nc.scalar.copy, nc.vector.tensor_copy)[r](result[:], acc[:])
             nc.sync.dma_start(out[:, r * RH : (r + 1) * RH], result[:])

@@ -49,6 +49,10 @@ def tile_picked_ysembl_wst_p_kernel(
         unit_sb = keep.tile([P, PACK], F32, name="unit_sb")
         ident = keep.tile([P, P], F32, name="ident")
 
+        warm = keep.tile([P, 2], F32, name="warm")
+        nc.gpsimd.memset(warm[:, 0:1], 1.0)
+        nc.scalar.activation(warm[:, 1:2], warm[:, 0:1], ACT.Abs_reciprocal_sqrt)
+
         nc.vector.memset(scales[:].bitcast(I32), 0)
         nc.sync.dma_start(offs_sb[:], offs)
         w1_rows = w1.rearrange("(p j) c -> p j c", j=PACK)
@@ -69,9 +73,6 @@ def tile_picked_ysembl_wst_p_kernel(
         for t in (2, 3):
             nc.sync.dma_start(gains[t][:], st_rows[:, t, :])
         make_identity(nc, ident[:])
-
-        warm = keep.tile([P, 1], F32, name="warm")
-        nc.scalar.activation(warm[:], ident[:, 0:1], ACT.Abs_reciprocal_sqrt, bias=0.5, scale=4.0)
 
         w1_bf = keep.tile([P, PACK, P, PACK], BF16, name="w1_bf", align_bytes=64)
         for c, move in enumerate((nc.scalar.copy, nc.vector.tensor_copy)):
@@ -163,7 +164,7 @@ def tile_picked_ysembl_wst_p_kernel(
             nc.vector.tensor_tensor(part(t, 2), part(t, 1), root[:], ALU.mult)
 
         def weigh(t):
-            if t in (3,):
+            if t in (2, 3):
                 nc.vector.tensor_tensor(part(t, 3), part(t, 2), part(t, 2), ALU.mult)
             else:
                 nc.scalar.activation(part(t, 3), part(t, 2), ACT.Square)
@@ -202,31 +203,31 @@ def tile_picked_ysembl_wst_p_kernel(
         moveout(0, 0)
         moveout(0, 1)
         project(2)
+        stack_up(0)
         moveout(1, 0)
+        normalise(0)
         moveout(1, 1)
         project(3)
-        stack_up(0)
-        normalise(0)
-        weigh(0)
-        look_up(0, 0)
-        look_up(0, 1)
-        moveout(2, 0)
-        moveout(2, 1)
         stack_up(1)
+        weigh(0)
+        moveout(2, 0)
         normalise(1)
-        weigh(1)
-        look_up(1, 0)
-        look_up(1, 1)
-        moveout(3, 0)
-        moveout(3, 1)
+        moveout(2, 1)
         stack_up(2)
+        weigh(1)
+        moveout(3, 0)
         normalise(2)
-        weigh(2)
-        look_up(2, 0)
-        look_up(2, 1)
+        moveout(3, 1)
         stack_up(3)
+        weigh(2)
         normalise(3)
         weigh(3)
+        look_up(0, 0)
+        look_up(0, 1)
+        look_up(1, 0)
+        look_up(1, 1)
+        look_up(2, 0)
+        look_up(2, 1)
         look_up(3, 0)
         look_up(3, 1)
 

@@ -15,17 +15,19 @@ U8 = mybir.dt.uint8
 FP8X4 = mybir.dt.float8_e4m3fn_x4
 ALU = mybir.AluOpType
 ACT = mybir.ActivationFunctionType
-AXIS = mybir.AxisListType
 
 P = 128
 PACK = 4
+LANES = 16
+QUADRANT = 32
 HALF = S // 2
-VB = HALF // D
-RH = U // 2
+GROUPS = HALF // D
+OUT_HALF = U // 2
+STACK_ON_TENSOR = 2
 
 
 def entries(lst, a, b):
-    return lst[:, a // 16 : b // 16]
+    return lst[:, a // LANES : b // LANES]
 
 
 def tile_picked_ysembl_wst_p_kernel(
@@ -38,9 +40,9 @@ def tile_picked_ysembl_wst_p_kernel(
         psum_y = ctx.enter_context(tc.psum_pool(name="psum_y", bufs=3))
         psum_e = ctx.enter_context(tc.psum_pool(name="psum_e", bufs=2))
 
-        offs_sb = keep.tile([P, S // 16], U16, name="offs_sb")
-        mv_sb = keep.tile([P, S // 16], U16, name="mv_sb")
-        out_t_sb = keep.tile([P, U // 16], U16, name="out_t_sb")
+        offs_sb = keep.tile([P, S // LANES], U16, name="offs_sb")
+        mv_sb = keep.tile([P, S // LANES], U16, name="mv_sb")
+        out_t_sb = keep.tile([P, U // LANES], U16, name="out_t_sb")
         words = keep.tile([P, T], I32, name="words", align_bytes=64)
         scales = keep.tile([P, T], U8, name="scales", align_bytes=64)
         w1_raw = [keep.tile([P, PACK, H // 2], F32, name=f"w1_raw{c}") for c in range(2)]
@@ -54,23 +56,21 @@ def tile_picked_ysembl_wst_p_kernel(
         nc.scalar.activation(warm[:, 1:2], warm[:, 0:1], ACT.Abs_reciprocal_sqrt)
 
         nc.vector.memset(scales[:].bitcast(I32), 0)
-        nc.sync.dma_start(offs_sb[:], offs)
+
         w1_rows = w1.rearrange("(p j) c -> p j c", j=PACK)
+        st_rows = st.rearrange("(p t) j -> p t j", t=PACK)
+        nc.sync.dma_start(offs_sb[:], offs)
         for c in range(2):
             nc.sync.dma_start(w1_raw[c][:], w1_rows[:, :, c * (H // 2) : (c + 1) * (H // 2)])
         for q in range(4):
-            nc.sync.dma_start(
-                scales[32 * q : 32 * q + 4, :].bitcast(I32), x_scales[0][4 * q : 4 * q + 4, :].bitcast(I32)
-            )
+            nc.sync.dma_start(scales[q:P:QUADRANT, :].bitcast(I32), x_scales[0][q::4, :].bitcast(I32))
         nc.sync.dma_start(words[:], x_words[0].rearrange("p n t -> p (n t)").bitcast(I32))
         nc.sync.dma_start(mv_sb[:], mv)
         nc.sync.dma_start(w2_raw[:], w2.rearrange("(p j) m -> p j m", j=PACK))
-        st_rows = st.rearrange("(p t) j -> p t j", t=PACK)
-        for t in (0, 1):
-            nc.sync.dma_start(gains[t][:], st_rows[:, t, :])
-        nc.sync.dma_start(out_t_sb[:], out_t)
-        nc.sync.dma_start(unit_sb[:], unit.rearrange("(p t) o -> p (t o)", t=PACK))
-        for t in (2, 3):
+        for t in range(PACK):
+            if t == PACK // 2:
+                nc.sync.dma_start(out_t_sb[:], out_t)
+                nc.sync.dma_start(unit_sb[:], unit.rearrange("(p t) o -> p (t o)", t=PACK))
             nc.sync.dma_start(gains[t][:], st_rows[:, t, :])
         make_identity(nc, ident[:])
 
@@ -86,6 +86,7 @@ def tile_picked_ysembl_wst_p_kernel(
             out=w1_codes[:].bitcast(FP8X4), scales=w1_scales[:], in_=w1_bf[:].rearrange("p t m j -> p (t m j)")
         )
 
+        halves = ((0, HALF), (HALF, S))
         pieces = ((0, HALF), (HALF, 3 * S // 4), (3 * S // 4, S))
         x_bytes = keep.tile([P, S], U8, name="x_bytes", align_bytes=64)
         nc.vector.tensor_copy(x_bytes[:], scales[:].indirect(offs_sb[:]))
@@ -96,12 +97,14 @@ def tile_picked_ysembl_wst_p_kernel(
         y_sb = [keep.tile([P, S], F32, name=f"y{t}") for t in range(PACK)]
         flats = [keep.tile([P, S], F32, name=f"flat{t}") for t in range(PACK)]
         tables = [keep.tile([P, 4 * V], F32, name=f"table{t}") for t in range(PACK)]
-        hid_rows = [keep.tile([P, PACK, RH], BF16, name=f"hid_rows{r}") for r in range(2)]
-        ON_PE = (0, 1)
-        sums_t = {}
+        hid_rows = [keep.tile([P, PACK, OUT_HALF], BF16, name=f"hid_rows{r}") for r in range(2)]
+        sums = {}
+
+        def stretch(t, n):
+            return tables[t][:, n * V : (n + 1) * V]
 
         def project(t):
-            for a, b in pieces if t == 0 else ((0, HALF), (HALF, S)):
+            for a, b in pieces if t == 0 else halves:
                 acc = psum_y.tile([P, b - a], F32, name="acc")
                 nc.tensor.matmul_mx(
                     out=acc[:],
@@ -112,137 +115,113 @@ def tile_picked_ysembl_wst_p_kernel(
                     start=True,
                     stop=True,
                 )
-                if t == 0 and b == S:
-                    nc.vector.tensor_copy(y_sb[t][:, a:b], acc[:])
-                else:
-                    nc.scalar.copy(y_sb[t][:, a:b], acc[:])
+                move = nc.vector.tensor_copy if t == 0 and b == S else nc.scalar.copy
+                move(y_sb[t][:, a:b], acc[:])
 
-        def part(t, n):
-            return tables[t][:, n * V : (n + 1) * V]
-
-        def add_groups(dst, columns):
+        def add_groups(dst, member):
             for d in range(D):
                 nc.tensor.matmul(
-                    dst, lhsT=columns(d), rhs=ident[:], start=(d == 0), stop=(d == D - 1), is_transpose=True
+                    dst, lhsT=member(d), rhs=ident[:], start=(d == 0), stop=(d == D - 1), is_transpose=True
                 )
+
+        def transpose_back(src):
+            back = psum_e.tile([P, V], F32, name="back")
+            for n in range(2):
+                nc.tensor.transpose(back[:, n * GROUPS : (n + 1) * GROUPS], src[:, n * P : (n + 1) * P], ident[:])
+            return back
 
         def moveout(t, h):
             if h == 0:
-                sums_t[t] = psum_e.tile([P, 4, P], F32, name="sums_t", bufs=3)
-            a, b = h * HALF, (h + 1) * HALF
+                sums[t] = psum_e.tile([P, 4, P], F32, name="sums", bufs=3)
+            a, b = halves[h]
             flat = flats[t][:, a:b]
             nc.vector.tensor_tensor(flat, y_sb[t][:].indirect(entries(mv_sb, a, b)), gains[t][:, a:b], ALU.mult)
-            squares = ring.tile([P, HALF], F32, name="squares", bufs=4)
+            squares = ring.tile([P, 2, GROUPS, 2], F32, name="squares", bufs=4)
             nc.scalar.activation(
-                squares[:].rearrange("p (e v f) -> p v e f", e=2, f=2),
+                squares[:].rearrange("p e v f -> p v e f"),
                 flat.rearrange("p (v e f) -> p v e f", e=2, f=2),
                 ACT.Square,
             )
-            column = lambda d: squares[:, (d // 2) * 2 * VB + d % 2 : (d // 2 + 1) * 2 * VB : 2]
-            if t in ON_PE:
-                add_groups(sums_t[t][:, 2 + h, :], lambda d: flat[:, d::D])
-            add_groups(sums_t[t][:, h, :], column)
+            if t < STACK_ON_TENSOR:
+                add_groups(sums[t][:, 2 + h, :], lambda d: flat[:, d::D])
+            add_groups(sums[t][:, h, :], lambda d: squares[:, d // 2, :, d % 2])
 
         def stack_up(t):
-            if t in ON_PE:
-                return
             groups = flats[t][:].rearrange("p (v d) -> p v d", d=D)
             pairs = ring.tile([P, V, 2], F32, name="pairs")
             nc.vector.tensor_tensor(pairs[:], groups[:, :, 0:2], groups[:, :, 2:4], ALU.add)
-            nc.vector.tensor_tensor(part(t, 1), pairs[:, :, 0], pairs[:, :, 1], ALU.add)
+            nc.vector.tensor_tensor(stretch(t, 1), pairs[:, :, 0], pairs[:, :, 1], ALU.add)
 
         def normalise(t):
-            root_t = ring.tile([P, 2, P], F32, name="root_t")
-            nc.scalar.activation(root_t[:], sums_t[t][:, 0:2, :], ACT.Abs_reciprocal_sqrt, bias=0.5, scale=4.0)
-            if t in ON_PE:
-                stack_t = sums_t[t][:, 2:4, :].rearrange("p a b -> p (a b)")
-                nc.vector.tensor_tensor(part(t, 2), root_t[:].rearrange("p a b -> p (a b)"), stack_t, ALU.mult)
-                return
-            root = psum_e.tile([P, V], F32, name="root")
-            for h in range(2):
-                nc.tensor.transpose(root[:, h * VB : (h + 1) * VB], root_t[:, h, :], ident[:])
-            nc.vector.tensor_tensor(part(t, 2), part(t, 1), root[:], ALU.mult)
+            root = ring.tile([P, V], F32, name="root")
+            energ = sums[t][:, 0:2, :].rearrange("v n p -> v (n p)")
+            nc.scalar.activation(root[:], energ, ACT.Abs_reciprocal_sqrt, bias=0.5, scale=4.0)
+            if t < STACK_ON_TENSOR:
+                stack = sums[t][:, 2:4, :].rearrange("v n p -> v (n p)")
+                nc.vector.tensor_tensor(stretch(t, 2), root[:], stack, ALU.mult)
+            else:
+                nc.vector.tensor_tensor(stretch(t, 2), stretch(t, 1), transpose_back(root)[:], ALU.mult)
 
         def weigh(t):
-            if t in (2, 3):
-                nc.vector.tensor_tensor(part(t, 3), part(t, 2), part(t, 2), ALU.mult)
+            gain = unit_sb[:, t : t + 1]
+            if t < STACK_ON_TENSOR:
+                nc.scalar.activation(stretch(t, 3), stretch(t, 2), ACT.Square)
+                stack = sums[t][:, 2:4, :].rearrange("v n p -> v (n p)")
+                nc.vector.tensor_tensor(stretch(t, 1), stretch(t, 3), stack, ALU.mult)
+                nc.scalar.activation(stretch(t, 0), transpose_back(stretch(t, 1))[:], ACT.Copy, scale=gain)
             else:
-                nc.scalar.activation(part(t, 3), part(t, 2), ACT.Square)
-            if t in ON_PE:
-                stack_t = sums_t[t][:, 2:4, :].rearrange("p a b -> p (a b)")
-                nc.vector.tensor_tensor(part(t, 1), part(t, 3), stack_t, ALU.mult)
-                back = psum_e.tile([P, V], F32, name="root")
-                for h in range(2):
-                    nc.tensor.transpose(back[:, h * VB : (h + 1) * VB], part(t, 1)[:, h * VB : (h + 1) * VB], ident[:])
-                nc.scalar.activation(part(t, 0), back[:], ACT.Copy, scale=unit_sb[:, t : t + 1])
-                return
-            nc.vector.scalar_tensor_tensor(part(t, 0), part(t, 3), unit_sb[:, t : t + 1], part(t, 1), ALU.mult, ALU.mult)
-
-        def look_up(t, r):
-            picked = tables[t][:].indirect(entries(out_t_sb, r * RH, (r + 1) * RH))
-            if (t, r) in ((3, 0),):
-                nc.vector.tensor_copy(hid_rows[r][:, t, :], picked)
-            else:
-                nc.scalar.activation(hid_rows[r][:, t, :], picked, ACT.Copy)
+                nc.vector.tensor_tensor(stretch(t, 3), stretch(t, 2), stretch(t, 2), ALU.mult)
+                nc.vector.scalar_tensor_tensor(stretch(t, 0), stretch(t, 3), gain, stretch(t, 1), ALU.mult, ALU.mult)
 
         w2_bf = keep.tile([P, N, PACK], BF16, name="w2_bf", align_bytes=64)
         w2_codes = keep.tile([P, N], U32, name="w2_codes", align_bytes=64)
         w2_scales = keep.tile([P, N], U8, name="w2_scales", align_bytes=64)
 
-        def second_weights():
-            nc.scalar.copy(
-                w2_bf[:].rearrange("p (c i) j -> p c j i", i=4), w2_raw[:].rearrange("p j (c i) -> p c j i", i=4)
-            )
-            nc.vector.quantize_mx(
-                out=w2_codes[:].bitcast(FP8X4), scales=w2_scales[:], in_=w2_bf[:].rearrange("p m j -> p (m j)")
-            )
+        ahead = 2
+        for t in range(ahead):
+            project(t)
 
-        project(0)
-        project(1)
-        second_weights()
-        moveout(0, 0)
-        moveout(0, 1)
-        project(2)
-        stack_up(0)
-        moveout(1, 0)
-        normalise(0)
-        moveout(1, 1)
-        project(3)
-        stack_up(1)
-        weigh(0)
-        moveout(2, 0)
-        normalise(1)
-        moveout(2, 1)
-        stack_up(2)
-        weigh(1)
-        moveout(3, 0)
-        normalise(2)
-        moveout(3, 1)
-        stack_up(3)
-        weigh(2)
-        normalise(3)
-        weigh(3)
-        look_up(0, 0)
-        look_up(0, 1)
-        look_up(1, 0)
-        look_up(1, 1)
-        look_up(2, 0)
-        look_up(2, 1)
-        look_up(3, 0)
-        look_up(3, 1)
+        nc.scalar.copy(
+            w2_bf[:].rearrange("p (c i) j -> p c j i", i=4), w2_raw[:].rearrange("p j (c i) -> p c j i", i=4)
+        )
+        nc.vector.quantize_mx(
+            out=w2_codes[:].bitcast(FP8X4), scales=w2_scales[:], in_=w2_bf[:].rearrange("p m j -> p (m j)")
+        )
 
-        for r in range(2):
-            hid_bf = keep.tile([P, RH, PACK], BF16, name=f"hid_bf{r}", align_bytes=64)
-            (nc.scalar.copy if r in () else nc.vector.tensor_copy)(
+        for t in range(PACK):
+            moveout(t, 0)
+            if t > 0:
+                normalise(t - 1)
+            moveout(t, 1)
+            if t + ahead < PACK:
+                project(t + ahead)
+            if t >= STACK_ON_TENSOR:
+                stack_up(t)
+            if t > 0:
+                weigh(t - 1)
+        normalise(PACK - 1)
+        weigh(PACK - 1)
+
+        for t in range(PACK):
+            for r in range(2):
+                picked = tables[t][:].indirect(entries(out_t_sb, r * OUT_HALF, (r + 1) * OUT_HALF))
+                if t == PACK - 1 and r == 0:
+                    nc.vector.tensor_copy(hid_rows[r][:, t, :], picked)
+                else:
+                    nc.scalar.activation(hid_rows[r][:, t, :], picked, ACT.Copy)
+
+        for r, move in enumerate((nc.scalar.copy, nc.vector.tensor_copy)):
+            hid_bf = keep.tile([P, OUT_HALF, PACK], BF16, name=f"hid_bf{r}", align_bytes=64)
+            nc.vector.tensor_copy(
                 hid_bf[:].rearrange("p (c i) t -> p c t i", i=4),
                 hid_rows[r][:].rearrange("p t (c i) -> p c t i", i=4),
             )
-            hid_codes = keep.tile([P, RH], U32, name=f"hid_codes{r}", align_bytes=64)
-            hid_scales = keep.tile([P, RH], U8, name=f"hid_scales{r}", align_bytes=64)
+            hid_codes = keep.tile([P, OUT_HALF], U32, name=f"hid_codes{r}", align_bytes=64)
+            hid_scales = keep.tile([P, OUT_HALF], U8, name=f"hid_scales{r}", align_bytes=64)
             nc.vector.quantize_mx(
-                out=hid_codes[:].bitcast(FP8X4), scales=hid_scales[:], in_=hid_bf[:].rearrange("p r t -> p (r t)")
+                out=hid_codes[:].bitcast(FP8X4), scales=hid_scales[:], in_=hid_bf[:].rearrange("p c t -> p (c t)")
             )
-            acc = psum_y.tile([P, RH], F32, name="acc")
+            acc = psum_y.tile([P, OUT_HALF], F32, name="acc")
             nc.tensor.matmul_mx(
                 out=acc[:],
                 lhsT=w2_codes[:].bitcast(FP8X4),
@@ -252,6 +231,6 @@ def tile_picked_ysembl_wst_p_kernel(
                 start=True,
                 stop=True,
             )
-            result = keep.tile([P, RH], F32, name=f"result{r}")
-            (nc.scalar.copy, nc.vector.tensor_copy)[r](result[:], acc[:])
-            nc.sync.dma_start(out[:, r * RH : (r + 1) * RH], result[:])
+            result = keep.tile([P, OUT_HALF], F32, name=f"result{r}")
+            move(result[:], acc[:])
+            nc.sync.dma_start(out[:, r * OUT_HALF : (r + 1) * OUT_HALF], result[:])

from contextlib import ExitStack

import concourse.mybir as mybir
from concourse.masks import make_identity

K, T, S, D, N, H, V, U = 512, 4096, 1024, 4, 128, 512, 256, 512
FLOPS = 2 * K * H * S + 2 * H * N * U

F32 = mybir.dt.float32
BF16 = mybir.dt.bfloat16
I32 = mybir.dt.int32
U32 = mybir.dt.uint32
U16 = mybir.dt.uint16
U8 = mybir.dt.uint8
FP8X4 = mybir.dt.float8_e4m3fn_x4
ALU = mybir.AluOpType
ACT = mybir.ActivationFunctionType

P = 128
PACK = 4
LANES = 16
QUADRANT = 32
HALF = S // 2
GROUPS = HALF // D
OUT_HALF = U // 2
STACK_ON_TENSOR = 2


def entries(lst, a, b):
    return lst[:, a // LANES : b // LANES]


def tile_picked_ysembl_wst_p_kernel(
    tc, x_words, x_scales, w1, st, unit, w2, offs, mv, out_t, out
):
    nc = tc.nc
    with ExitStack() as ctx:
        keep = ctx.enter_context(tc.tile_pool(name="keep", bufs=1))
        ring = ctx.enter_context(tc.tile_pool(name="ring", bufs=2))
        psum_y = ctx.enter_context(tc.psum_pool(name="psum_y", bufs=3))
        psum_e = ctx.enter_context(tc.psum_pool(name="psum_e", bufs=2))

        offs_sb = keep.tile([P, S // LANES], U16, name="offs_sb")
        mv_sb = keep.tile([P, S // LANES], U16, name="mv_sb")
        out_t_sb = keep.tile([P, U // LANES], U16, name="out_t_sb")
        words = keep.tile([P, T], I32, name="words", align_bytes=64)
        scales = keep.tile([P, T], U8, name="scales", align_bytes=64)
        w1_raw = [keep.tile([P, PACK, H // 2], F32, name=f"w1_raw{c}") for c in range(2)]
        w2_raw = keep.tile([P, PACK, N], F32, name="w2_raw")
        gains = [keep.tile([P, S], F32, name=f"gains{t}") for t in range(PACK)]
        unit_sb = keep.tile([P, PACK], F32, name="unit_sb")
        ident = keep.tile([P, P], F32, name="ident")

        warm = keep.tile([P, 2], F32, name="warm")
        nc.gpsimd.memset(warm[:, 0:1], 1.0)
        nc.scalar.activation(warm[:, 1:2], warm[:, 0:1], ACT.Abs_reciprocal_sqrt)

        nc.vector.memset(scales[:].bitcast(I32), 0)

        w1_rows = w1.rearrange("(p j) c -> p j c", j=PACK)
        st_rows = st.rearrange("(p t) j -> p t j", t=PACK)
        nc.sync.dma_start(offs_sb[:], offs)
        for c in range(2):
            nc.sync.dma_start(w1_raw[c][:], w1_rows[:, :, c * (H // 2) : (c + 1) * (H // 2)])
        for q in range(4):
            nc.sync.dma_start(scales[q:P:QUADRANT, :].bitcast(I32), x_scales[0][q::4, :].bitcast(I32))
        nc.sync.dma_start(words[:], x_words[0].rearrange("p n t -> p (n t)").bitcast(I32))
        nc.sync.dma_start(mv_sb[:], mv)
        nc.sync.dma_start(w2_raw[:], w2.rearrange("(p j) m -> p j m", j=PACK))
        for t in range(PACK):
            if t == PACK // 2:
                nc.sync.dma_start(out_t_sb[:], out_t)
                nc.sync.dma_start(unit_sb[:], unit.rearrange("(p t) o -> p (t o)", t=PACK))
            nc.sync.dma_start(gains[t][:], st_rows[:, t, :])
        make_identity(nc, ident[:])

        w1_bf = keep.tile([P, PACK, P, PACK], BF16, name="w1_bf", align_bytes=64)
        for c, move in enumerate((nc.scalar.copy, nc.vector.tensor_copy)):
            move(
                w1_bf[:, :, c * (P // 2) : (c + 1) * (P // 2), :].rearrange("p t m j -> p m t j"),
                w1_raw[c][:].rearrange("p j (m t) -> p m t j", t=PACK),
            )
        w1_codes = keep.tile([P, H], U32, name="w1_codes", align_bytes=64)
        w1_scales = keep.tile([P, H], U8, name="w1_scales", align_bytes=64)
        nc.vector.quantize_mx(
            out=w1_codes[:].bitcast(FP8X4), scales=w1_scales[:], in_=w1_bf[:].rearrange("p t m j -> p (t m j)")
        )

        halves = ((0, HALF), (HALF, S))
        pieces = ((0, HALF), (HALF, 3 * S // 4), (3 * S // 4, S))
        x_bytes = keep.tile([P, S], U8, name="x_bytes", align_bytes=64)
        nc.vector.tensor_copy(x_bytes[:], scales[:].indirect(offs_sb[:]))
        x_codes = keep.tile([P, S], U32, name="x_codes", align_bytes=64)
        for a, b in pieces:
            nc.vector.tensor_copy(x_codes[:, a:b], words[:].bitcast(U32).indirect(entries(offs_sb, a, b)))

        y_sb = [keep.tile([P, S], F32, name=f"y{t}") for t in range(PACK)]
        flats = [keep.tile([P, S], F32, name=f"flat{t}") for t in range(PACK)]
        tables = [keep.tile([P, 4 * V], F32, name=f"table{t}") for t in range(PACK)]
        hid_rows = [keep.tile([P, PACK, OUT_HALF], BF16, name=f"hid_rows{r}") for r in range(2)]
        sums = {}

        def stretch(t, n):
            return tables[t][:, n * V : (n + 1) * V]

        def project(t):
            for a, b in pieces if t == 0 else halves:
                acc = psum_y.tile([P, b - a], F32, name="acc")
                nc.tensor.matmul_mx(
                    out=acc[:],
                    lhsT=w1_codes[:, t * P : (t + 1) * P].bitcast(FP8X4),
                    lhsT_scale=w1_scales[:, t * P : (t + 1) * P],
                    rhs=x_codes[:, a:b].bitcast(FP8X4),
                    rhs_scale=x_bytes[:, a:b],
                    start=True,
                    stop=True,
                )
                move = nc.vector.tensor_copy if t == 0 and b == S else nc.scalar.copy
                move(y_sb[t][:, a:b], acc[:])

        def add_groups(dst, member):
            for d in range(D):
                nc.tensor.matmul(
                    dst, lhsT=member(d), rhs=ident[:], start=(d == 0), stop=(d == D - 1), is_transpose=True
                )

        def transpose_back(src):
            back = psum_e.tile([P, V], F32, name="back")
            for n in range(2):
                nc.tensor.transpose(back[:, n * GROUPS : (n + 1) * GROUPS], src[:, n * P : (n + 1) * P], ident[:])
            return back

        def moveout(t, h):
            if h == 0:
                sums[t] = psum_e.tile([P, 4, P], F32, name="sums", bufs=3)
            a, b = halves[h]
            flat = flats[t][:, a:b]
            nc.vector.tensor_tensor(flat, y_sb[t][:].indirect(entries(mv_sb, a, b)), gains[t][:, a:b], ALU.mult)
            squares = ring.tile([P, 2, GROUPS, 2], F32, name="squares", bufs=4)
            nc.scalar.activation(
                squares[:].rearrange("p e v f -> p v e f"),
                flat.rearrange("p (v e f) -> p v e f", e=2, f=2),
                ACT.Square,
            )
            if t < STACK_ON_TENSOR:
                add_groups(sums[t][:, 2 + h, :], lambda d: flat[:, d::D])
            add_groups(sums[t][:, h, :], lambda d: squares[:, d // 2, :, d % 2])

        def stack_up(t):
            groups = flats[t][:].rearrange("p (v d) -> p v d", d=D)
            pairs = ring.tile([P, V, 2], F32, name="pairs")
            nc.vector.tensor_tensor(pairs[:], groups[:, :, 0:2], groups[:, :, 2:4], ALU.add)
            nc.vector.tensor_tensor(stretch(t, 1), pairs[:, :, 0], pairs[:, :, 1], ALU.add)

        def normalise(t):
            root = ring.tile([P, V], F32, name="root")
            energ = sums[t][:, 0:2, :].rearrange("v n p -> v (n p)")
            nc.scalar.activation(root[:], energ, ACT.Abs_reciprocal_sqrt, bias=0.5, scale=4.0)
            if t < STACK_ON_TENSOR:
                stack = sums[t][:, 2:4, :].rearrange("v n p -> v (n p)")
                nc.vector.tensor_tensor(stretch(t, 2), root[:], stack, ALU.mult)
            else:
                nc.vector.tensor_tensor(stretch(t, 2), stretch(t, 1), transpose_back(root)[:], ALU.mult)

        def weigh(t):
            gain = unit_sb[:, t : t + 1]
            if t < STACK_ON_TENSOR:
                nc.scalar.activation(stretch(t, 3), stretch(t, 2), ACT.Square)
                stack = sums[t][:, 2:4, :].rearrange("v n p -> v (n p)")
                nc.vector.tensor_tensor(stretch(t, 1), stretch(t, 3), stack, ALU.mult)
                nc.scalar.activation(stretch(t, 0), transpose_back(stretch(t, 1))[:], ACT.Copy, scale=gain)
            else:
                nc.vector.tensor_tensor(stretch(t, 3), stretch(t, 2), stretch(t, 2), ALU.mult)
                nc.vector.scalar_tensor_tensor(stretch(t, 0), stretch(t, 3), gain, stretch(t, 1), ALU.mult, ALU.mult)

        w2_bf = keep.tile([P, N, PACK], BF16, name="w2_bf", align_bytes=64)
        w2_codes = keep.tile([P, N], U32, name="w2_codes", align_bytes=64)
        w2_scales = keep.tile([P, N], U8, name="w2_scales", align_bytes=64)

        ahead = 2
        for t in range(ahead):
            project(t)

        nc.scalar.copy(
            w2_bf[:].rearrange("p (c i) j -> p c j i", i=4), w2_raw[:].rearrange("p j (c i) -> p c j i", i=4)
        )
        nc.vector.quantize_mx(
            out=w2_codes[:].bitcast(FP8X4), scales=w2_scales[:], in_=w2_bf[:].rearrange("p m j -> p (m j)")
        )

        for t in range(PACK):
            moveout(t, 0)
            if t > 0:
                normalise(t - 1)
            moveout(t, 1)
            if t + ahead < PACK:
                project(t + ahead)
            if t >= STACK_ON_TENSOR:
                stack_up(t)
            if t > 0:
                weigh(t - 1)
        normalise(PACK - 1)
        weigh(PACK - 1)

        for t in range(PACK):
            for r in range(2):
                picked = tables[t][:].indirect(entries(out_t_sb, r * OUT_HALF, (r + 1) * OUT_HALF))
                if t == PACK - 1 and r == 0:
                    nc.vector.tensor_copy(hid_rows[r][:, t, :], picked)
                else:
                    nc.scalar.activation(hid_rows[r][:, t, :], picked, ACT.Copy)

        for r, move in enumerate((nc.scalar.copy, nc.vector.tensor_copy)):
            hid_bf = keep.tile([P, OUT_HALF, PACK], BF16, name=f"hid_bf{r}", align_bytes=64)
            nc.vector.tensor_copy(
                hid_bf[:].rearrange("p (c i) t -> p c t i", i=4),
                hid_rows[r][:].rearrange("p t (c i) -> p c t i", i=4),
            )
            hid_codes = keep.tile([P, OUT_HALF], U32, name=f"hid_codes{r}", align_bytes=64)
            hid_scales = keep.tile([P, OUT_HALF], U8, name=f"hid_scales{r}", align_bytes=64)
            nc.vector.quantize_mx(
                out=hid_codes[:].bitcast(FP8X4), scales=hid_scales[:], in_=hid_bf[:].rearrange("p c t -> p (c t)")
            )
            acc = psum_y.tile([P, OUT_HALF], F32, name="acc")
            nc.tensor.matmul_mx(
                out=acc[:],
                lhsT=w2_codes[:].bitcast(FP8X4),
                lhsT_scale=w2_scales[:],
                rhs=hid_codes[:].bitcast(FP8X4),
                rhs_scale=hid_scales[:],
                start=True,
                stop=True,
            )
            result = keep.tile([P, OUT_HALF], F32, name=f"result{r}")
            move(result[:], acc[:])
            nc.sync.dma_start(out[:, r * OUT_HALF : (r + 1) * OUT_HALF], result[:])
